import numpy as np
import ml_dtypes


def mxq(x, axis, fmt="e4m3"):
    dtype, down = {"e4m3": (ml_dtypes.float8_e4m3fn, 7), "e5m2": (ml_dtypes.float8_e5m2, 14)}[fmt]
    v = np.moveaxis(np.asarray(x, np.float32).astype(ml_dtypes.bfloat16).astype(np.float64), axis, -1)
    blocks = v.reshape(v.shape[:-1] + (-1, 32))
    amax = np.abs(blocks).max(-1, keepdims=True)
    byte = np.maximum(np.where(amax > 0, np.frexp(amax)[1] - 1 + 127, 0) - down, 1)
    scale = np.exp2(byte - 127.0)
    codes = (blocks / scale).astype(np.float32).astype(dtype).astype(np.float64)
    return np.moveaxis((codes * scale).reshape(v.shape), -1, axis)


WIDE = False


def mx_kscale(k):
    if not WIDE:
        return np.ones(k)
    levels = np.array([10, -10, 5, -5, 0])
    if k % 512:
        return np.exp2(np.random.permutation(np.resize(levels, k // 32))).repeat(32)
    a = np.empty((k // 512, 16))
    for p in range(k // 512):
        a[p, :8] = np.random.permutation(np.resize(levels, 8))
        for g in range(8):
            far = levels[np.abs(levels - a[p, g]) >= 10]
            a[p, g + 8] = far[np.random.randint(len(far))]
    return np.exp2(a.ravel()).repeat(32)


def f64(x):
    return np.asarray(x).astype(np.float64)


def striped(idx):
    return np.tile(np.asarray(idx).reshape(-1, 16).T, (8, 1)).astype(np.uint16)


def unstriped(offs):
    return offs[:16].T.reshape(-1).astype(np.int64)


E2M1 = np.array([0.0, 0.5, 1.0, 1.5, 2.0, 3.0, 4.0, 6.0, -0.0, -0.5, -1.0, -1.5, -2.0, -3.0, -4.0, -6.0])


def pack_weight(w, fmt):
    k, n = w.shape
    w = f64(np.asarray(w, np.float32).astype(ml_dtypes.bfloat16)).reshape(k // 32, 32, n)
    amax = np.abs(w).max(1)
    if fmt == "e4m3":
        byte = np.frexp(amax)[1] - 1 + 127 - 7
    else:
        mant, ex = np.frexp(amax / 6.0)
        byte = np.where(mant > 0.5, ex, ex - 1) + 127
    byte = np.clip(np.where(amax > 0, byte, 1), 1, 254)
    scaled = (w * np.exp2(127.0 - byte)[:, None, :]).reshape(k, n).astype(np.float32)
    by_word = np.ascontiguousarray(scaled.reshape(k // 512, 128, 4, n).transpose(0, 1, 3, 2))
    if fmt == "e4m3":
        words = by_word.astype(ml_dtypes.float8_e4m3fn).view(np.uint8)
    else:
        c = by_word.astype(ml_dtypes.float4_e2m1fn).view(np.uint8) & 0xF
        words = (c[..., 0::2] | (c[..., 1::2] << 4)).reshape(k // 512, 128, 2 * n)
    return np.ascontiguousarray(words), np.ascontiguousarray(byte.astype(np.uint8).reshape(k // 512, 16, n))


def unpack_weight(words, scales, fmt):
    g, _, n = scales.shape
    words = np.ascontiguousarray(words).reshape(g, 128, n, -1)
    if fmt == "e4m3":
        vals = words.view(ml_dtypes.float8_e4m3fn).astype(np.float64)
    else:
        nib = np.empty((g, 128, n, 4), np.uint8)
        nib[..., 0::2] = words & 0xF
        nib[..., 1::2] = words >> 4
        vals = E2M1[nib]
    vals = vals * np.repeat(np.exp2(scales.astype(np.float64) - 127.0), 8, axis=1)[..., None]
    return vals.transpose(0, 1, 3, 2).reshape(g * 512, n)


K, T, J, R, N = 512, 1024, 128, 512, 512


def setup_inputs():
    n = np.random.standard_normal
    idx = np.random.permutation(T)[:J]
    fk = mx_kscale(K)
    fr = mx_kscale(R)
    xqp = pack_weight(n((K, T)) / fk[:, None], "e4m3")
    w1p = pack_weight(n((K, R)) * 1 / np.sqrt(K) * fk[:, None] * fr, "e2m1")
    wxp = pack_weight(n((R, N)) * 1 / np.sqrt(R) / fr[:, None], "e4m3")
    wbp = pack_weight(n((R, N)) * 1 / np.sqrt(R) / fr[:, None], "e2m1")
    return {
        "xq_words": xqp[0],
        "xq_scales": xqp[1],
        "w1_words": w1p[0],
        "w1_scales": w1p[1],
        "wx_words": wxp[0],
        "wx_scales": wxp[1],
        "wb_words": wbp[0],
        "wb_scales": wbp[1],
        "offs": striped(idx),
    }


def reference(xq_words, xq_scales, w1_words, w1_scales, wx_words, wx_scales, wb_words, wb_scales, offs):
    idx = unstriped(offs)
    xqu = unpack_weight(xq_words, xq_scales, "e4m3")
    w1u = unpack_weight(w1_words, w1_scales, "e2m1")
    wxu = unpack_weight(wx_words, wx_scales, "e4m3")
    wbu = unpack_weight(wb_words, wb_scales, "e2m1")
    a = w1u.T @ xqu
    hid = np.maximum(a, 0.0)
    hidq = mxq(hid, 0, "e4m3")
    e = wxu.T @ hidq
    hididxq = mxq(hid[:, idx], 0, "e4m3")
    p = wbu.T @ hididxq
    d = 4.0 * np.maximum(p, 0.0)
    dp = np.zeros((N, T))
    dp[:, idx] = d
    y = e + dp
    return y

@@ -1,0 +1,210 @@
+from contextlib import ExitStack
+
+import concourse.mybir as mybir
+
+K, T, J, R, N = 512, 1024, 128, 512, 512
+FLOPS = 2 * K * R * T + 2 * R * N * T + 2 * R * N * J
+
+F32 = mybir.dt.float32
+BF16 = mybir.dt.bfloat16
+I32 = mybir.dt.int32
+U32 = mybir.dt.uint32
+U16 = mybir.dt.uint16
+U8 = mybir.dt.uint8
+FP8X4 = mybir.dt.float8_e4m3fn_x4
+FP4X4 = mybir.dt.float4_e2m1fn_x4
+RELU = mybir.ActivationFunctionType.Relu
+COPY = mybir.ActivationFunctionType.Copy
+ADD = mybir.AluOpType.add
+
+P = 128
+PACK = 4
+CHUNK = 128
+CHUNKS = T // CHUNK
+HALF = T // 2
+N_TILES = N // P
+
+
+def load_scales(queue, plane, scales):
+    for q in range(4):
+        queue.dma_start(out=plane[32 * q : 32 * q + 4, :].bitcast(I32), in_=scales[0, 4 * q : 4 * q + 4, :].bitcast(I32))
+
+
+def spread_scales(queue, plane, scales, q):
+    rows = scales[0, 4 * q : 4 * q + 4, :].bitcast(I32)
+    queue.dma_start(out=plane[32 * q : 32 * q + 32, :].bitcast(I32), in_=rows.partition_broadcast(8))
+
+
+def tile_list_stay_or_leave_kernel(tc, xq_words, xq_scales, w1_words, w1_scales, wx_words, wx_scales, wb_words, wb_scales, offs, out):
+    nc = tc.nc
+    with ExitStack() as ctx:
+        keep = ctx.enter_context(tc.tile_pool(name="keep", bufs=1))
+        psum = ctx.enter_context(tc.psum_pool(name="psum", bufs=1))
+
+        offsets = keep.tile([P, J // 16], U16, name="offsets")
+        w1_raw = keep.tile([P, 2 * R], U8, name="w1_raw", align_bytes=64)
+        w1_raw_s = keep.tile([P, R], U8, name="w1_raw_s", align_bytes=64)
+        w1_c = keep.tile([P, 2 * R], U8, name="w1_c", align_bytes=64)
+        w1_s = keep.tile([P, R], U8, name="w1_s", align_bytes=64)
+        x_c = [keep.tile([P, HALF], U32, name="x_c%d" % h, align_bytes=64) for h in range(2)]
+        x_s = keep.tile([P, T], U8, name="x_s", align_bytes=64)
+        wx_c = keep.tile([P, N], U32, name="wx_c", align_bytes=64)
+        wx_s = keep.tile([P, N], U8, name="wx_s", align_bytes=64)
+        wb_c = keep.tile([P, 2 * N], U8, name="wb_c", align_bytes=64)
+        wb_s = keep.tile([P, N], U8, name="wb_s", align_bytes=64)
+        hid = keep.tile([P, PACK, T], F32, name="hid", align_bytes=64)
+        h_b = [keep.tile([P, CHUNK, PACK], BF16, name="h_b%d" % c, align_bytes=64) for c in range(CHUNKS)]
+        h_c = [keep.tile([P, HALF], U32, name="h_c%d" % h, align_bytes=64) for h in range(2)]
+        h_s = [keep.tile([P, HALF], U8, name="h_s%d" % h, align_bytes=64) for h in range(2)]
+        g_b = keep.tile([P, J, PACK], BF16, name="g_b", align_bytes=64)
+        g_c = keep.tile([P, J], U32, name="g_c", align_bytes=64)
+        g_s = keep.tile([P, J], U8, name="g_s", align_bytes=64)
+        d = keep.tile([P, N_TILES, J], F32, name="d", align_bytes=64)
+        dp = [keep.tile([P, T], F32, name="dp%d" % n, align_bytes=64) for n in range(N_TILES)]
+        e_sb = [keep.tile([P, HALF], F32, name="e_sb%d" % n, align_bytes=64) for n in range(N_TILES)]
+        y = [[keep.tile([P, HALF], F32, name="y%d_%d" % (n, h), align_bytes=64) for h in range(2)] for n in range(N_TILES)]
+        warm = keep.tile([P, 8], F32, name="warm")
+
+        xw = xq_words[0].rearrange("p c r -> p (c r)")
+        spread_scales(nc.sync, w1_raw_s, w1_scales, 0)
+        spread_scales(nc.scalar, x_s, xq_scales, 0)
+        spread_scales(nc.sync, w1_raw_s, w1_scales, 1)
+        nc.scalar.dma_start(out=w1_raw[:].bitcast(I32), in_=w1_words[0].bitcast(I32))
+        spread_scales(nc.sync, w1_raw_s, w1_scales, 2)
+        spread_scales(nc.scalar, x_s, xq_scales, 1)
+        spread_scales(nc.sync, w1_raw_s, w1_scales, 3)
+        nc.scalar.dma_start(out=x_c[0][:].bitcast(I32), in_=xw[:, 0 : 4 * HALF].bitcast(I32))
+        spread_scales(nc.sync, x_s, xq_scales, 2)
+        spread_scales(nc.sync, x_s, xq_scales, 3)
+        nc.gpsimd.memset(warm[:], 0.0)
+        nc.gpsimd.memset(wx_s[:].bitcast(I32), 0)
+        nc.gpsimd.memset(wb_s[:].bitcast(I32), 0)
+        nc.scalar.activation(warm[:, 4:5], warm[:, 0:1], RELU)
+        nc.sync.dma_start(out=x_c[1][:].bitcast(I32), in_=xw[:, 4 * HALF : 4 * T].bitcast(I32))
+        nc.sync.dma_start(offsets[:], offs)
+        nc.sync.dma_start(out=wx_c[:].bitcast(I32), in_=wx_words[0].rearrange("p c r -> p (c r)").bitcast(I32))
+        load_scales(nc.sync, wx_s, wx_scales)
+        nc.sync.dma_start(out=wb_c[:].bitcast(I32), in_=wb_words[0].bitcast(I32))
+        load_scales(nc.sync, wb_s, wb_scales)
+        for n in range(N_TILES - 1):
+            nc.vector.memset(dp[n][:], 0.0)
+
+        nc.vector.tensor_copy(
+            out=w1_s[:].rearrange("p (j m) -> p j m", j=PACK),
+            in_=w1_raw_s[:].rearrange("p (m j) -> p j m", j=PACK),
+        )
+        nc.vector.tensor_copy(
+            out=w1_c[:].bitcast(U16).rearrange("p (j m) -> p j m", j=PACK),
+            in_=w1_raw[:].bitcast(U16).rearrange("p (m j) -> p j m", j=PACK),
+        )
+        nc.vector.memset(dp[N_TILES - 1][:], 0.0)
+
+        def bank(b, shape, name):
+            return psum.tile(shape, F32, name=name, tag="bank%d" % b)
+
+        a = []
+        for c in range(CHUNKS):
+            acc = bank(c, [P, PACK, CHUNK], "a%d" % c)
+            a.append(acc)
+            h, o = divmod(c * CHUNK, HALF)
+            for j in range(PACK):
+                nc.tensor.matmul_mx(
+                    out=acc[:, j, :],
+                    lhsT=w1_c[:, 2 * P * j : 2 * P * (j + 1)].bitcast(FP4X4),
+                    lhsT_scale=w1_s[:, P * j : P * (j + 1)],
+                    rhs=x_c[h][:, o : o + CHUNK].bitcast(FP8X4),
+                    rhs_scale=x_s[:, c * CHUNK : (c + 1) * CHUNK],
+                    start=True,
+                    stop=True,
+                )
+
+        def keep_hid(c):
+            dst = hid[:, :, c * CHUNK : (c + 1) * CHUNK]
+            nc.scalar.activation(dst, a[c][:], RELU)
+
+        def round_from_sbuf(c):
+            nc.vector.tensor_copy(
+                out=h_b[c][:],
+                in_=hid[:, :, c * CHUNK : (c + 1) * CHUNK].rearrange("p j t -> p t j"),
+            )
+
+        def round_from_psum(c):
+            nc.scalar.activation(h_b[c][:], a[c][:].rearrange("p j t -> p t j"), RELU)
+
+        def quantise(c):
+            h, o = divmod(c * CHUNK, HALF)
+            nc.vector.quantize_mx(
+                out=h_c[h][:, o : o + CHUNK].bitcast(FP8X4),
+                scales=h_s[h][:, o : o + CHUNK],
+                in_=h_b[c][:].rearrange("p t j -> p (t j)"),
+            )
+
+        for c in range(6):
+            keep_hid(c)
+            round_from_sbuf(c)
+            if c > 0:
+                quantise(c - 1)
+        keep_hid(6)
+        keep_hid(7)
+
+        def exit_product(n, h, b):
+            acc = bank(b, [P, HALF], "e%d_%d" % (n, h))
+            nc.tensor.matmul_mx(
+                out=acc[:],
+                lhsT=wx_c[:, P * n : P * (n + 1)].bitcast(FP8X4),
+                lhsT_scale=wx_s[:, P * n : P * (n + 1)],
+                rhs=h_c[h][:].bitcast(FP8X4),
+                rhs_scale=h_s[h][:],
+                start=True,
+                stop=True,
+            )
+            return acc
+
+        e0 = [exit_product(n, 0, n) for n in range(N_TILES)]
+
+        for j in range(PACK):
+            nc.vector.tensor_copy(out=g_b[:, :, j], in_=hid[:, j, :].indirect(offsets[:]))
+        for c in range(6, CHUNKS):
+            round_from_psum(c)
+        quantise(5)
+        nc.vector.quantize_mx(out=g_c[:].bitcast(FP8X4), scales=g_s[:], in_=g_b[:].rearrange("p t j -> p (t j)"))
+        pacc = bank(4, [P, N_TILES, J], "pacc")
+        for n in range(N_TILES):
+            nc.tensor.matmul_mx(
+                out=pacc[:, n, :],
+                lhsT=wb_c[:, 2 * P * n : 2 * P * (n + 1)].bitcast(FP4X4),
+                lhsT_scale=wb_s[:, P * n : P * (n + 1)],
+                rhs=g_c[:].bitcast(FP8X4),
+                rhs_scale=g_s[:],
+                start=True,
+                stop=True,
+            )
+        for c in range(6, CHUNKS):
+            quantise(c)
+        nc.scalar.activation(d[:], pacc[:], RELU, scale=4.0)
+        e1 = [exit_product(n, 1, 4 + (n + 1) % 4) for n in range(N_TILES)]
+
+        def scatter(n):
+            nc.vector.tensor_copy(out=dp[n][:].indirect(offsets[:]), in_=d[:, n, :])
+
+        def finish_low(n):
+            nc.scalar.activation(e_sb[n][:], e0[n][:], COPY)
+            nc.gpsimd.tensor_tensor(y[n][0][:], e_sb[n][:], dp[n][:, 0:HALF], ADD)
+            nc.sync.dma_start(out=out[P * n : P * (n + 1), 0:HALF], in_=y[n][0][:])
+
+        def finish_high(n):
+            nc.vector.tensor_tensor(y[n][1][:], e1[n][:], dp[n][:, HALF:T], ADD)
+            nc.sync.dma_start(out=out[P * n : P * (n + 1), HALF:T], in_=y[n][1][:])
+
+        scatter(0)
+        finish_high(0)
+        finish_low(0)
+        scatter(1)
+        finish_low(1)
+        scatter(2)
+        finish_high(1)
+        finish_low(2)
+        scatter(3)
+        finish_high(2)
+        finish_low(3)
+        finish_high(3)

@@ -42,8 +42,8 @@ def tile_list_stay_or_leave_kernel(tc, xq_words, xq_scales, w1_words, w1_scales,
         psum = ctx.enter_context(tc.psum_pool(name="psum", bufs=1))
 
         offsets = keep.tile([P, J // 16], U16, name="offsets")
-        w1_raw = keep.tile([P, 2 * R], U8, name="w1_raw", align_bytes=64)
-        w1_raw_s = keep.tile([P, R], U8, name="w1_raw_s", align_bytes=64)
+        w1_raw = keep.tile([P, 2 * R], U8, name="w1_raw", tag="dp2", align_bytes=64)
+        w1_raw_s = keep.tile([P, R], U8, name="w1_raw_s", tag="dp3", align_bytes=64)
         w1_c = keep.tile([P, 2 * R], U8, name="w1_c", align_bytes=64)
         w1_s = keep.tile([P, R], U8, name="w1_s", align_bytes=64)
         x_c = [keep.tile([P, HALF], U32, name="x_c%d" % h, align_bytes=64) for h in range(2)]
@@ -53,15 +53,13 @@ def tile_list_stay_or_leave_kernel(tc, xq_words, xq_scales, w1_words, w1_scales,
         wb_c = keep.tile([P, 2 * N], U8, name="wb_c", align_bytes=64)
         wb_s = keep.tile([P, N], U8, name="wb_s", align_bytes=64)
         hid = keep.tile([P, PACK, T], F32, name="hid", align_bytes=64)
-        h_b = [keep.tile([P, CHUNK, PACK], BF16, name="h_b%d" % c, align_bytes=64) for c in range(CHUNKS)]
+        h_b = [keep.tile([P, HALF * PACK], BF16, name="h_b%d" % h, align_bytes=64) for h in range(2)]
         h_c = [keep.tile([P, HALF], U32, name="h_c%d" % h, align_bytes=64) for h in range(2)]
         h_s = [keep.tile([P, HALF], U8, name="h_s%d" % h, align_bytes=64) for h in range(2)]
         g_b = keep.tile([P, J, PACK], BF16, name="g_b", align_bytes=64)
-        g_c = keep.tile([P, J], U32, name="g_c", align_bytes=64)
+        g_c = keep.tile([P, J], U32, name="g_c", tag="e_sb", align_bytes=64)
         g_s = keep.tile([P, J], U8, name="g_s", align_bytes=64)
         d = keep.tile([P, N_TILES, J], F32, name="d", align_bytes=64)
-        dp = [keep.tile([P, T], F32, name="dp%d" % n, align_bytes=64) for n in range(N_TILES)]
-        e_sb = [keep.tile([P, HALF], F32, name="e_sb%d" % n, align_bytes=64) for n in range(N_TILES)]
         y = [[keep.tile([P, HALF], F32, name="y%d_%d" % (n, h), align_bytes=64) for h in range(2)] for n in range(N_TILES)]
         warm = keep.tile([P, 8], F32, name="warm")
 
@@ -86,8 +84,15 @@ def tile_list_stay_or_leave_kernel(tc, xq_words, xq_scales, w1_words, w1_scales,
         load_scales(nc.sync, wx_s, wx_scales)
         nc.sync.dma_start(out=wb_c[:].bitcast(I32), in_=wb_words[0].bitcast(I32))
         load_scales(nc.sync, wb_s, wb_scales)
-        for n in range(N_TILES - 1):
-            nc.vector.memset(dp[n][:], 0.0)
+        dp = []
+
+        def clear_page(n):
+            page = keep.tile([P, T], F32, name="dp%d" % n, tag="dp%d" % n, align_bytes=64)
+            nc.vector.memset(page[:].bitcast(I32), 0)
+            dp.append(page)
+
+        clear_page(0)
+        clear_page(1)
 
         nc.vector.tensor_copy(
             out=w1_s[:].rearrange("p (j m) -> p j m", j=PACK),
@@ -97,55 +102,60 @@ def tile_list_stay_or_leave_kernel(tc, xq_words, xq_scales, w1_words, w1_scales,
             out=w1_c[:].bitcast(U16).rearrange("p (j m) -> p j m", j=PACK),
             in_=w1_raw[:].bitcast(U16).rearrange("p (m j) -> p j m", j=PACK),
         )
-        nc.vector.memset(dp[N_TILES - 1][:], 0.0)
+        clear_page(2)
+        clear_page(3)
 
         def bank(b, shape, name):
             return psum.tile(shape, F32, name=name, tag="bank%d" % b)
 
-        a = []
-        for c in range(CHUNKS):
-            acc = bank(c, [P, PACK, CHUNK], "a%d" % c)
-            a.append(acc)
-            h, o = divmod(c * CHUNK, HALF)
-            for j in range(PACK):
-                nc.tensor.matmul_mx(
-                    out=acc[:, j, :],
-                    lhsT=w1_c[:, 2 * P * j : 2 * P * (j + 1)].bitcast(FP4X4),
-                    lhsT_scale=w1_s[:, P * j : P * (j + 1)],
-                    rhs=x_c[h][:, o : o + CHUNK].bitcast(FP8X4),
-                    rhs_scale=x_s[:, c * CHUNK : (c + 1) * CHUNK],
-                    start=True,
-                    stop=True,
-                )
-
-        def keep_hid(c):
-            dst = hid[:, :, c * CHUNK : (c + 1) * CHUNK]
-            nc.scalar.activation(dst, a[c][:], RELU)
-
-        def round_from_sbuf(c):
-            nc.vector.tensor_copy(
-                out=h_b[c][:],
-                in_=hid[:, :, c * CHUNK : (c + 1) * CHUNK].rearrange("p j t -> p t j"),
+        def first_product(dst, j, h, o, width):
+            nc.tensor.matmul_mx(
+                out=dst,
+                lhsT=w1_c[:, 2 * P * j : 2 * P * (j + 1)].bitcast(FP4X4),
+                lhsT_scale=w1_s[:, P * j : P * (j + 1)],
+                rhs=x_c[h][:, o : o + width].bitcast(FP8X4),
+                rhs_scale=x_s[:, h * HALF + o : h * HALF + o + width],
+                start=True,
+                stop=True,
             )
 
-        def round_from_psum(c):
-            nc.scalar.activation(h_b[c][:], a[c][:].rearrange("p j t -> p t j"), RELU)
-
-        def quantise(c):
+        def woven(c):
             h, o = divmod(c * CHUNK, HALF)
+            return (
+                h_b[h][:, PACK * o : PACK * (o + CHUNK)].rearrange("p (t j) -> p t j", j=PACK),
+                hid[:, :, c * CHUNK : (c + 1) * CHUNK].rearrange("p j t -> p t j"),
+            )
+
+        def weave_vector(c):
+            dst, src = woven(c)
+            nc.vector.tensor_copy(out=dst, in_=src)
+
+        def weave_scalar(c):
+            dst, src = woven(c)
+            nc.scalar.activation(dst, src, COPY)
+
+        def quantise(h, o, width):
             nc.vector.quantize_mx(
-                out=h_c[h][:, o : o + CHUNK].bitcast(FP8X4),
-                scales=h_s[h][:, o : o + CHUNK],
-                in_=h_b[c][:].rearrange("p t j -> p (t j)"),
+                out=h_c[h][:, o : o + width].bitcast(FP8X4),
+                scales=h_s[h][:, o : o + width],
+                in_=h_b[h][:, PACK * o : PACK * (o + width)],
             )
 
-        for c in range(6):
-            keep_hid(c)
-            round_from_sbuf(c)
-            if c > 0:
-                quantise(c - 1)
-        keep_hid(6)
-        keep_hid(7)
+        for c in range(4):
+            acc = bank(c, [P, PACK, CHUNK], "a%d" % c)
+            for j in range(PACK):
+                first_product(acc[:, j, :], j, 0, c * CHUNK, CHUNK)
+            nc.scalar.activation(hid[:, :, c * CHUNK : (c + 1) * CHUNK], acc[:], RELU)
+            weave_vector(c)
+            if c == 2:
+                quantise(0, 0, 2 * CHUNK)
+        for j in range(PACK):
+            acc = bank(4 + j, [P, HALF], "a%d" % (4 + j))
+            first_product(acc[:], j, 1, 0, HALF)
+            nc.scalar.activation(hid[:, j, HALF:T], acc[:], RELU)
+            nc.vector.tensor_copy(out=g_b[:, :, j], in_=hid[:, j, :].indirect(offsets[:]))
+            if j == 0:
+                quantise(0, 2 * CHUNK, 2 * CHUNK)
 
         def exit_product(n, h, b):
             acc = bank(b, [P, HALF], "e%d_%d" % (n, h))
@@ -161,17 +171,14 @@ def tile_list_stay_or_leave_kernel(tc, xq_words, xq_scales, w1_words, w1_scales,
             return acc
 
         e0 = [exit_product(n, 0, n) for n in range(N_TILES)]
-
-        for j in range(PACK):
-            nc.vector.tensor_copy(out=g_b[:, :, j], in_=hid[:, j, :].indirect(offsets[:]))
-        for c in range(6, CHUNKS):
-            round_from_psum(c)
-        quantise(5)
+        weave_scalar(4)
+        weave_scalar(5)
         nc.vector.quantize_mx(out=g_c[:].bitcast(FP8X4), scales=g_s[:], in_=g_b[:].rearrange("p t j -> p (t j)"))
-        pacc = bank(4, [P, N_TILES, J], "pacc")
+        p_first = bank(4, [P, J], "p_first")
+        p_rest = bank(5, [P, N_TILES - 1, J], "p_rest")
         for n in range(N_TILES):
             nc.tensor.matmul_mx(
-                out=pacc[:, n, :],
+                out=p_first[:] if n == 0 else p_rest[:, n - 1, :],
                 lhsT=wb_c[:, 2 * P * n : 2 * P * (n + 1)].bitcast(FP4X4),
                 lhsT_scale=wb_s[:, P * n : P * (n + 1)],
                 rhs=g_c[:].bitcast(FP8X4),
@@ -179,17 +186,22 @@ def tile_list_stay_or_leave_kernel(tc, xq_words, xq_scales, w1_words, w1_scales,
                 start=True,
                 stop=True,
             )
-        for c in range(6, CHUNKS):
-            quantise(c)
-        nc.scalar.activation(d[:], pacc[:], RELU, scale=4.0)
-        e1 = [exit_product(n, 1, 4 + (n + 1) % 4) for n in range(N_TILES)]
+        weave_vector(6)
+        weave_vector(7)
+        quantise(1, 0, HALF)
+        nc.scalar.activation(d[:, 0, :], p_first[:], RELU, scale=4.0)
+        nc.scalar.activation(d[:, 1:, :], p_rest[:], RELU, scale=4.0)
+
+        e_first = keep.tile([P, HALF], F32, name="e_first", align_bytes=64)
+        e_rest = keep.tile([P, N_TILES - 1, HALF], F32, name="e_rest", tag="e_sb", align_bytes=64)
+        e_sb = [e_first[:]] + [e_rest[:, n, :] for n in range(N_TILES - 1)]
 
         def scatter(n):
             nc.vector.tensor_copy(out=dp[n][:].indirect(offsets[:]), in_=d[:, n, :])
 
         def finish_low(n):
-            nc.scalar.activation(e_sb[n][:], e0[n][:], COPY)
-            nc.gpsimd.tensor_tensor(y[n][0][:], e_sb[n][:], dp[n][:, 0:HALF], ADD)
+            nc.scalar.activation(e_sb[n], e0[n][:], COPY)
+            nc.gpsimd.tensor_tensor(y[n][0][:], e_sb[n], dp[n][:, 0:HALF], ADD)
             nc.sync.dma_start(out=out[P * n : P * (n + 1), 0:HALF], in_=y[n][0][:])
 
         def finish_high(n):
@@ -197,6 +209,7 @@ def tile_list_stay_or_leave_kernel(tc, xq_words, xq_scales, w1_words, w1_scales,
             nc.sync.dma_start(out=out[P * n : P * (n + 1), HALF:T], in_=y[n][1][:])
 
         scatter(0)
+        e1 = [exit_product(n, 1, 4 + (n + 2) % 4) for n in range(N_TILES)]
         finish_high(0)
         finish_low(0)
         scatter(1)

@@ -173,6 +173,7 @@ def tile_list_stay_or_leave_kernel(tc, xq_words, xq_scales, w1_words, w1_scales,
         e0 = [exit_product(n, 0, n) for n in range(N_TILES)]
         weave_scalar(4)
         weave_scalar(5)
+        weave_vector(6)
         nc.vector.quantize_mx(out=g_c[:].bitcast(FP8X4), scales=g_s[:], in_=g_b[:].rearrange("p t j -> p (t j)"))
         p_first = bank(4, [P, J], "p_first")
         p_rest = bank(5, [P, N_TILES - 1, J], "p_rest")
@@ -186,38 +187,38 @@ def tile_list_stay_or_leave_kernel(tc, xq_words, xq_scales, w1_words, w1_scales,
                 start=True,
                 stop=True,
             )
-        weave_vector(6)
         weave_vector(7)
         quantise(1, 0, HALF)
         nc.scalar.activation(d[:, 0, :], p_first[:], RELU, scale=4.0)
         nc.scalar.activation(d[:, 1:, :], p_rest[:], RELU, scale=4.0)
 
-        e_first = keep.tile([P, HALF], F32, name="e_first", align_bytes=64)
-        e_rest = keep.tile([P, N_TILES - 1, HALF], F32, name="e_rest", tag="e_sb", align_bytes=64)
-        e_sb = [e_first[:]] + [e_rest[:, n, :] for n in range(N_TILES - 1)]
+        e_sb = keep.tile([P, 2, HALF], F32, name="e_sb", tag="e_sb", align_bytes=64)
 
         def scatter(n):
             nc.vector.tensor_copy(out=dp[n][:].indirect(offsets[:]), in_=d[:, n, :])
 
-        def finish_low(n):
-            nc.scalar.activation(e_sb[n], e0[n][:], COPY)
-            nc.gpsimd.tensor_tensor(y[n][0][:], e_sb[n], dp[n][:, 0:HALF], ADD)
-            nc.sync.dma_start(out=out[P * n : P * (n + 1), 0:HALF], in_=y[n][0][:])
+        def store(n, h):
+            nc.sync.dma_start(out=out[P * n : P * (n + 1), h * HALF : (h + 1) * HALF], in_=y[n][h][:])
 
-        def finish_high(n):
-            nc.vector.tensor_tensor(y[n][1][:], e1[n][:], dp[n][:, HALF:T], ADD)
-            nc.sync.dma_start(out=out[P * n : P * (n + 1), HALF:T], in_=y[n][1][:])
+        def finish_on_gpsimd(n):
+            nc.scalar.activation(e_sb[:, n, :], e[0][n][:], COPY)
+            nc.gpsimd.tensor_tensor(y[n][0][:], e_sb[:, n, :], dp[n][:, 0:HALF], ADD)
+            store(n, 0)
 
+        def finish_on_vector(n, h):
+            nc.vector.tensor_tensor(y[n][h][:], e[h][n][:], dp[n][:, h * HALF : (h + 1) * HALF], ADD)
+            store(n, h)
+
+        e = [e0, [exit_product(n, 1, 4 + (n + 2) % 4) for n in range(N_TILES)]]
         scatter(0)
-        e1 = [exit_product(n, 1, 4 + (n + 2) % 4) for n in range(N_TILES)]
-        finish_high(0)
-        finish_low(0)
         scatter(1)
-        finish_low(1)
+        finish_on_gpsimd(0)
+        finish_on_vector(0, 1)
+        finish_on_vector(1, 1)
         scatter(2)
-        finish_high(1)
-        finish_low(2)
+        finish_on_gpsimd(1)
+        finish_on_vector(2, 0)
+        finish_on_vector(2, 1)
         scatter(3)
-        finish_high(2)
-        finish_low(3)
-        finish_high(3)
+        finish_on_vector(3, 0)
+        finish_on_vector(3, 1)

@@ -42,8 +42,9 @@ def tile_list_stay_or_leave_kernel(tc, xq_words, xq_scales, w1_words, w1_scales,
         psum = ctx.enter_context(tc.psum_pool(name="psum", bufs=1))
 
         offsets = keep.tile([P, J // 16], U16, name="offsets")
-        w1_raw = keep.tile([P, 2 * R], U8, name="w1_raw", tag="dp2", align_bytes=64)
-        w1_raw_s = keep.tile([P, R], U8, name="w1_raw_s", tag="dp3", align_bytes=64)
+        w1_stage = keep.tile([P, 3 * R], U8, name="w1_stage", tag="dp3", align_bytes=64)
+        w1_raw = w1_stage[:, 0 : 2 * R]
+        w1_raw_s = w1_stage[:, 2 * R : 3 * R]
         w1_c = keep.tile([P, 2 * R], U8, name="w1_c", align_bytes=64)
         w1_s = keep.tile([P, R], U8, name="w1_s", align_bytes=64)
         x_c = [keep.tile([P, HALF], U32, name="x_c%d" % h, align_bytes=64) for h in range(2)]
@@ -59,25 +60,21 @@ def tile_list_stay_or_leave_kernel(tc, xq_words, xq_scales, w1_words, w1_scales,
         g_b = keep.tile([P, J, PACK], BF16, name="g_b", align_bytes=64)
         g_c = keep.tile([P, J], U32, name="g_c", tag="e_sb", align_bytes=64)
         g_s = keep.tile([P, J], U8, name="g_s", align_bytes=64)
-        d = keep.tile([P, N_TILES, J], F32, name="d", align_bytes=64)
         y = [[keep.tile([P, HALF], F32, name="y%d_%d" % (n, h), align_bytes=64) for h in range(2)] for n in range(N_TILES)]
-        warm = keep.tile([P, 8], F32, name="warm")
 
         xw = xq_words[0].rearrange("p c r -> p (c r)")
         spread_scales(nc.sync, w1_raw_s, w1_scales, 0)
         spread_scales(nc.scalar, x_s, xq_scales, 0)
         spread_scales(nc.sync, w1_raw_s, w1_scales, 1)
-        nc.scalar.dma_start(out=w1_raw[:].bitcast(I32), in_=w1_words[0].bitcast(I32))
+        nc.scalar.dma_start(out=w1_raw.bitcast(I32), in_=w1_words[0].bitcast(I32))
         spread_scales(nc.sync, w1_raw_s, w1_scales, 2)
         spread_scales(nc.scalar, x_s, xq_scales, 1)
         spread_scales(nc.sync, w1_raw_s, w1_scales, 3)
         nc.scalar.dma_start(out=x_c[0][:].bitcast(I32), in_=xw[:, 0 : 4 * HALF].bitcast(I32))
         spread_scales(nc.sync, x_s, xq_scales, 2)
         spread_scales(nc.sync, x_s, xq_scales, 3)
-        nc.gpsimd.memset(warm[:], 0.0)
         nc.gpsimd.memset(wx_s[:].bitcast(I32), 0)
         nc.gpsimd.memset(wb_s[:].bitcast(I32), 0)
-        nc.scalar.activation(warm[:, 4:5], warm[:, 0:1], RELU)
         nc.sync.dma_start(out=x_c[1][:].bitcast(I32), in_=xw[:, 4 * HALF : 4 * T].bitcast(I32))
         nc.sync.dma_start(offsets[:], offs)
         nc.sync.dma_start(out=wx_c[:].bitcast(I32), in_=wx_words[0].rearrange("p c r -> p (c r)").bitcast(I32))
@@ -86,24 +83,24 @@ def tile_list_stay_or_leave_kernel(tc, xq_words, xq_scales, w1_words, w1_scales,
         load_scales(nc.sync, wb_s, wb_scales)
         dp = []
 
-        def clear_page(n):
+        def clear_page(engine, n):
             page = keep.tile([P, T], F32, name="dp%d" % n, tag="dp%d" % n, align_bytes=64)
-            nc.vector.memset(page[:].bitcast(I32), 0)
+            engine.memset(page[:].bitcast(I32), 0)
             dp.append(page)
 
-        clear_page(0)
-        clear_page(1)
+        clear_page(nc.vector, 0)
+        clear_page(nc.vector, 1)
+        clear_page(nc.gpsimd, 2)
 
         nc.vector.tensor_copy(
             out=w1_s[:].rearrange("p (j m) -> p j m", j=PACK),
-            in_=w1_raw_s[:].rearrange("p (m j) -> p j m", j=PACK),
+            in_=w1_raw_s.rearrange("p (m j) -> p j m", j=PACK),
         )
         nc.vector.tensor_copy(
             out=w1_c[:].bitcast(U16).rearrange("p (j m) -> p j m", j=PACK),
-            in_=w1_raw[:].bitcast(U16).rearrange("p (m j) -> p j m", j=PACK),
+            in_=w1_raw.bitcast(U16).rearrange("p (m j) -> p j m", j=PACK),
         )
-        clear_page(2)
-        clear_page(3)
+        clear_page(nc.vector, 3)
 
         def bank(b, shape, name):
             return psum.tile(shape, F32, name=name, tag="bank%d" % b)
@@ -152,7 +149,10 @@ def tile_list_stay_or_leave_kernel(tc, xq_words, xq_scales, w1_words, w1_scales,
         for j in range(PACK):
             acc = bank(4 + j, [P, HALF], "a%d" % (4 + j))
             first_product(acc[:], j, 1, 0, HALF)
-            nc.scalar.activation(hid[:, j, HALF:T], acc[:], RELU)
+            if j == 0:
+                nc.vector.tensor_scalar_max(hid[:, j, HALF:T], acc[:], 0.0)
+            else:
+                nc.scalar.activation(hid[:, j, HALF:T], acc[:], RELU)
             nc.vector.tensor_copy(out=g_b[:, :, j], in_=hid[:, j, :].indirect(offsets[:]))
             if j == 0:
                 quantise(0, 2 * CHUNK, 2 * CHUNK)
@@ -170,13 +170,14 @@ def tile_list_stay_or_leave_kernel(tc, xq_words, xq_scales, w1_words, w1_scales,
             )
             return acc
 
-        e0 = [exit_product(n, 0, n) for n in range(N_TILES)]
+        e = {(0, 0): exit_product(0, 0, 2)}
         weave_scalar(4)
         weave_scalar(5)
-        weave_vector(6)
+        weave_scalar(6)
+        weave_vector(7)
         nc.vector.quantize_mx(out=g_c[:].bitcast(FP8X4), scales=g_s[:], in_=g_b[:].rearrange("p t j -> p (t j)"))
-        p_first = bank(4, [P, J], "p_first")
-        p_rest = bank(5, [P, N_TILES - 1, J], "p_rest")
+        p_first = bank(0, [P, J], "p_first")
+        p_rest = bank(1, [P, N_TILES - 1, J], "p_rest")
         for n in range(N_TILES):
             nc.tensor.matmul_mx(
                 out=p_first[:] if n == 0 else p_rest[:, n - 1, :],
@@ -187,38 +188,41 @@ def tile_list_stay_or_leave_kernel(tc, xq_words, xq_scales, w1_words, w1_scales,
                 start=True,
                 stop=True,
             )
-        weave_vector(7)
         quantise(1, 0, HALF)
-        nc.scalar.activation(d[:, 0, :], p_first[:], RELU, scale=4.0)
-        nc.scalar.activation(d[:, 1:, :], p_rest[:], RELU, scale=4.0)
 
         e_sb = keep.tile([P, 2, HALF], F32, name="e_sb", tag="e_sb", align_bytes=64)
 
         def scatter(n):
-            nc.vector.tensor_copy(out=dp[n][:].indirect(offsets[:]), in_=d[:, n, :])
+            d = keep.tile([P, J], F32, name="d%d" % n, tag="d%d" % min(n, 1), align_bytes=64)
+            nc.scalar.activation(d[:], p_first[:] if n == 0 else p_rest[:, n - 1, :], RELU, scale=4.0)
+            nc.vector.tensor_copy(out=dp[n][:].indirect(offsets[:]), in_=d[:])
 
-        def store(n, h):
-            nc.sync.dma_start(out=out[P * n : P * (n + 1), h * HALF : (h + 1) * HALF], in_=y[n][h][:])
+        def store(queue, n, h):
+            queue.dma_start(out=out[P * n : P * (n + 1), h * HALF : (h + 1) * HALF], in_=y[n][h][:])
 
         def finish_on_gpsimd(n):
-            nc.scalar.activation(e_sb[:, n, :], e[0][n][:], COPY)
-            nc.gpsimd.tensor_tensor(y[n][0][:], e_sb[:, n, :], dp[n][:, 0:HALF], ADD)
-            store(n, 0)
+            nc.scalar.activation(e_sb[:, n // 2, :], e[n, 0][:], COPY)
+            nc.gpsimd.tensor_tensor(y[n][0][:], e_sb[:, n // 2, :], dp[n][:, 0:HALF], ADD)
+            store(nc.sync if n == 0 else nc.scalar, n, 0)
 
         def finish_on_vector(n, h):
-            nc.vector.tensor_tensor(y[n][h][:], e[h][n][:], dp[n][:, h * HALF : (h + 1) * HALF], ADD)
-            store(n, h)
+            nc.vector.tensor_tensor(y[n][h][:], e[n, h][:], dp[n][:, h * HALF : (h + 1) * HALF], ADD)
+            store(nc.sync, n, h)
 
-        e = [e0, [exit_product(n, 1, 4 + (n + 2) % 4) for n in range(N_TILES)]]
         scatter(0)
+        e[1, 0] = exit_product(1, 0, 0)
+        for n in range(N_TILES):
+            e[n, 1] = exit_product(n, 1, 4 + n)
         scatter(1)
         finish_on_gpsimd(0)
+        e[2, 0] = exit_product(2, 0, 2)
+        finish_on_vector(1, 0)
         finish_on_vector(0, 1)
-        finish_on_vector(1, 1)
         scatter(2)
-        finish_on_gpsimd(1)
-        finish_on_vector(2, 0)
+        finish_on_gpsimd(2)
+        finish_on_vector(1, 1)
         finish_on_vector(2, 1)
         scatter(3)
-        finish_on_vector(3, 0)
+        e[3, 0] = exit_product(3, 0, 1)
         finish_on_vector(3, 1)
+        finish_on_vector(3, 0)

@@ -19,23 +19,33 @@ ADD = mybir.AluOpType.add
 
 P = 128
 PACK = 4
+QUADRANT = 32
 CHUNK = 128
-CHUNKS = T // CHUNK
-HALF = T // 2
+QUARTER = 256
+LINE = 4
+HALF = 512
 N_TILES = N // P
 
 
-def load_scales(queue, plane, scales):
-    for q in range(4):
-        queue.dma_start(out=plane[32 * q : 32 * q + 4, :].bitcast(I32), in_=scales[0, 4 * q : 4 * q + 4, :].bitcast(I32))
+def load_scale_rows(queue, scale_tile, scales):
+    for q in range(P // QUADRANT):
+        queue.dma_start(
+            out=scale_tile[QUADRANT * q : QUADRANT * q + 4, :].bitcast(I32),
+            in_=scales[0, 4 * q : 4 * q + 4, :].bitcast(I32),
+        )
 
 
-def spread_scales(queue, plane, scales, q):
+def load_scale_quadrant(queue, scale_tile, scales, q):
     rows = scales[0, 4 * q : 4 * q + 4, :].bitcast(I32)
-    queue.dma_start(out=plane[32 * q : 32 * q + 32, :].bitcast(I32), in_=rows.partition_broadcast(8))
+    queue.dma_start(
+        out=scale_tile[QUADRANT * q : QUADRANT * (q + 1), :].bitcast(I32),
+        in_=rows.partition_broadcast(QUADRANT // 4),
+    )
 
 
-def tile_list_stay_or_leave_kernel(tc, xq_words, xq_scales, w1_words, w1_scales, wx_words, wx_scales, wb_words, wb_scales, offs, out):
+def tile_list_stay_or_leave_kernel(
+    tc, xq_words, xq_scales, w1_words, w1_scales, wx_words, wx_scales, wb_words, wb_scales, offs, out
+):
     nc = tc.nc
     with ExitStack() as ctx:
         keep = ctx.enter_context(tc.tile_pool(name="keep", bufs=1))
@@ -43,7 +53,7 @@ def tile_list_stay_or_leave_kernel(tc, xq_words, xq_scales, w1_words, w1_scales,
 
         offsets = keep.tile([P, J // 16], U16, name="offsets")
         w1_stage = keep.tile([P, 3 * R], U8, name="w1_stage", tag="dp3", align_bytes=64)
-        w1_raw = w1_stage[:, 0 : 2 * R]
+        w1_raw_c = w1_stage[:, 0 : 2 * R]
         w1_raw_s = w1_stage[:, 2 * R : 3 * R]
         w1_c = keep.tile([P, 2 * R], U8, name="w1_c", align_bytes=64)
         w1_s = keep.tile([P, R], U8, name="w1_s", align_bytes=64)
@@ -54,33 +64,37 @@ def tile_list_stay_or_leave_kernel(tc, xq_words, xq_scales, w1_words, w1_scales,
         wb_c = keep.tile([P, 2 * N], U8, name="wb_c", align_bytes=64)
         wb_s = keep.tile([P, N], U8, name="wb_s", align_bytes=64)
         hid = keep.tile([P, PACK, T], F32, name="hid", align_bytes=64)
-        h_b = [keep.tile([P, HALF * PACK], BF16, name="h_b%d" % h, align_bytes=64) for h in range(2)]
+        h_b = [keep.tile([P, QUARTER * PACK], BF16, name="h_b%d" % u, align_bytes=64) for u in range(3)]
         h_c = [keep.tile([P, HALF], U32, name="h_c%d" % h, align_bytes=64) for h in range(2)]
         h_s = [keep.tile([P, HALF], U8, name="h_s%d" % h, align_bytes=64) for h in range(2)]
-        g_b = keep.tile([P, J, PACK], BF16, name="g_b", align_bytes=64)
-        g_c = keep.tile([P, J], U32, name="g_c", tag="e_sb", align_bytes=64)
-        g_s = keep.tile([P, J], U8, name="g_s", align_bytes=64)
-        y = [[keep.tile([P, HALF], F32, name="y%d_%d" % (n, h), align_bytes=64) for h in range(2)] for n in range(N_TILES)]
+        picked_b = keep.tile([P, J, PACK], BF16, name="picked_b", tag="h_b3", align_bytes=64)
+        picked_c = keep.tile([P, J], U32, name="picked_c", tag="e_sb", align_bytes=64)
+        picked_s = keep.tile([P, J], U8, name="picked_s", align_bytes=64)
+        y = [
+            [keep.tile([P, HALF], F32, name="y%d_%d" % (n, h), align_bytes=64) for h in range(2)]
+            for n in range(N_TILES)
+        ]
 
-        xw = xq_words[0].rearrange("p c r -> p (c r)")
-        spread_scales(nc.sync, w1_raw_s, w1_scales, 0)
-        spread_scales(nc.scalar, x_s, xq_scales, 0)
-        spread_scales(nc.sync, w1_raw_s, w1_scales, 1)
-        nc.scalar.dma_start(out=w1_raw.bitcast(I32), in_=w1_words[0].bitcast(I32))
-        spread_scales(nc.sync, w1_raw_s, w1_scales, 2)
-        spread_scales(nc.scalar, x_s, xq_scales, 1)
-        spread_scales(nc.sync, w1_raw_s, w1_scales, 3)
-        nc.scalar.dma_start(out=x_c[0][:].bitcast(I32), in_=xw[:, 0 : 4 * HALF].bitcast(I32))
-        spread_scales(nc.sync, x_s, xq_scales, 2)
-        spread_scales(nc.sync, x_s, xq_scales, 3)
+        x_bytes = xq_words[0].rearrange("p c r -> p (c r)")
+        load_scale_quadrant(nc.sync, w1_raw_s, w1_scales, 0)
+        load_scale_quadrant(nc.scalar, x_s, xq_scales, 0)
+        load_scale_quadrant(nc.sync, w1_raw_s, w1_scales, 1)
+        nc.scalar.dma_start(out=w1_raw_c.bitcast(I32), in_=w1_words[0].bitcast(I32))
+        load_scale_quadrant(nc.sync, w1_raw_s, w1_scales, 2)
+        load_scale_quadrant(nc.scalar, x_s, xq_scales, 1)
+        load_scale_quadrant(nc.sync, w1_raw_s, w1_scales, 3)
+        nc.scalar.dma_start(out=x_c[0][:].bitcast(I32), in_=x_bytes[:, 0 : PACK * HALF].bitcast(I32))
+        load_scale_quadrant(nc.sync, x_s, xq_scales, 2)
+        load_scale_quadrant(nc.sync, x_s, xq_scales, 3)
         nc.gpsimd.memset(wx_s[:].bitcast(I32), 0)
         nc.gpsimd.memset(wb_s[:].bitcast(I32), 0)
-        nc.sync.dma_start(out=x_c[1][:].bitcast(I32), in_=xw[:, 4 * HALF : 4 * T].bitcast(I32))
+        nc.sync.dma_start(out=x_c[1][:].bitcast(I32), in_=x_bytes[:, PACK * HALF : PACK * T].bitcast(I32))
         nc.sync.dma_start(offsets[:], offs)
         nc.sync.dma_start(out=wx_c[:].bitcast(I32), in_=wx_words[0].rearrange("p c r -> p (c r)").bitcast(I32))
-        load_scales(nc.sync, wx_s, wx_scales)
+        load_scale_rows(nc.sync, wx_s, wx_scales)
         nc.sync.dma_start(out=wb_c[:].bitcast(I32), in_=wb_words[0].bitcast(I32))
-        load_scales(nc.sync, wb_s, wb_scales)
+        load_scale_rows(nc.sync, wb_s, wb_scales)
+
         dp = []
 
         def clear_page(engine, n):
@@ -98,64 +112,66 @@ def tile_list_stay_or_leave_kernel(tc, xq_words, xq_scales, w1_words, w1_scales,
         )
         nc.vector.tensor_copy(
             out=w1_c[:].bitcast(U16).rearrange("p (j m) -> p j m", j=PACK),
-            in_=w1_raw.bitcast(U16).rearrange("p (m j) -> p j m", j=PACK),
+            in_=w1_raw_c.bitcast(U16).rearrange("p (m j) -> p j m", j=PACK),
         )
         clear_page(nc.vector, 3)
 
         def bank(b, shape, name):
             return psum.tile(shape, F32, name=name, tag="bank%d" % b)
 
-        def first_product(dst, j, h, o, width):
+        def first_product(dst, j, h, start, width):
             nc.tensor.matmul_mx(
                 out=dst,
                 lhsT=w1_c[:, 2 * P * j : 2 * P * (j + 1)].bitcast(FP4X4),
                 lhsT_scale=w1_s[:, P * j : P * (j + 1)],
-                rhs=x_c[h][:, o : o + width].bitcast(FP8X4),
-                rhs_scale=x_s[:, h * HALF + o : h * HALF + o + width],
+                rhs=x_c[h][:, start : start + width].bitcast(FP8X4),
+                rhs_scale=x_s[:, h * HALF + start : h * HALF + start + width],
                 start=True,
                 stop=True,
             )
 
-        def woven(c):
-            h, o = divmod(c * CHUNK, HALF)
+        def woven(first, width):
+            u, start = divmod(first, QUARTER)
             return (
-                h_b[h][:, PACK * o : PACK * (o + CHUNK)].rearrange("p (t j) -> p t j", j=PACK),
-                hid[:, :, c * CHUNK : (c + 1) * CHUNK].rearrange("p j t -> p t j"),
+                h_b[u][:, PACK * start : PACK * (start + width)].rearrange("p (g i j) -> p g j i", i=LINE, j=PACK),
+                hid[:, :, first : first + width].rearrange("p j (g i) -> p g j i", i=LINE),
             )
 
-        def weave_vector(c):
-            dst, src = woven(c)
+        def weave_on_vector(first, width):
+            dst, src = woven(first, width)
             nc.vector.tensor_copy(out=dst, in_=src)
 
-        def weave_scalar(c):
-            dst, src = woven(c)
+        def weave_on_scalar(first, width):
+            dst, src = woven(first, width)
             nc.scalar.activation(dst, src, COPY)
 
-        def quantise(h, o, width):
+        def quantise(u):
+            h, start = divmod(u * QUARTER, HALF)
             nc.vector.quantize_mx(
-                out=h_c[h][:, o : o + width].bitcast(FP8X4),
-                scales=h_s[h][:, o : o + width],
-                in_=h_b[h][:, PACK * o : PACK * (o + width)],
+                out=h_c[h][:, start : start + QUARTER].bitcast(FP8X4),
+                scales=h_s[h][:, start : start + QUARTER],
+                in_=h_b[u][:],
             )
 
-        for c in range(4):
+        for c in range(HALF // CHUNK):
             acc = bank(c, [P, PACK, CHUNK], "a%d" % c)
             for j in range(PACK):
                 first_product(acc[:, j, :], j, 0, c * CHUNK, CHUNK)
             nc.scalar.activation(hid[:, :, c * CHUNK : (c + 1) * CHUNK], acc[:], RELU)
-            weave_vector(c)
+            weave_on_vector(c * CHUNK, CHUNK)
             if c == 2:
-                quantise(0, 0, 2 * CHUNK)
+                quantise(0)
+
         for j in range(PACK):
-            acc = bank(4 + j, [P, HALF], "a%d" % (4 + j))
+            acc = bank(HALF // CHUNK + j, [P, HALF], "a%d" % (HALF // CHUNK + j))
             first_product(acc[:], j, 1, 0, HALF)
             if j == 0:
                 nc.vector.tensor_scalar_max(hid[:, j, HALF:T], acc[:], 0.0)
             else:
                 nc.scalar.activation(hid[:, j, HALF:T], acc[:], RELU)
-            nc.vector.tensor_copy(out=g_b[:, :, j], in_=hid[:, j, :].indirect(offsets[:]))
+            nc.vector.tensor_copy(out=picked_b[:, :, j], in_=hid[:, j, :].indirect(offsets[:]))
             if j == 0:
-                quantise(0, 2 * CHUNK, 2 * CHUNK)
+                quantise(1)
 
         def exit_product(n, h, b):
             acc = bank(b, [P, HALF], "e%d_%d" % (n, h))
@@ -171,39 +187,43 @@ def tile_list_stay_or_leave_kernel(tc, xq_words, xq_scales, w1_words, w1_scales,
             return acc
 
         e = {(0, 0): exit_product(0, 0, 2)}
-        weave_scalar(4)
-        weave_scalar(5)
-        weave_scalar(6)
-        weave_vector(7)
-        nc.vector.quantize_mx(out=g_c[:].bitcast(FP8X4), scales=g_s[:], in_=g_b[:].rearrange("p t j -> p (t j)"))
+        weave_on_scalar(HALF, CHUNK)
+        weave_on_scalar(HALF + CHUNK, CHUNK)
+        nc.vector.quantize_mx(
+            out=picked_c[:].bitcast(FP8X4), scales=picked_s[:], in_=picked_b[:].rearrange("p t j -> p (t j)")
+        )
         p_first = bank(0, [P, J], "p_first")
         p_rest = bank(1, [P, N_TILES - 1, J], "p_rest")
+        p = [p_first[:]] + [p_rest[:, n, :] for n in range(N_TILES - 1)]
         for n in range(N_TILES):
             nc.tensor.matmul_mx(
-                out=p_first[:] if n == 0 else p_rest[:, n - 1, :],
+                out=p[n],
                 lhsT=wb_c[:, 2 * P * n : 2 * P * (n + 1)].bitcast(FP4X4),
                 lhsT_scale=wb_s[:, P * n : P * (n + 1)],
-                rhs=g_c[:].bitcast(FP8X4),
-                rhs_scale=g_s[:],
+                rhs=picked_c[:].bitcast(FP8X4),
+                rhs_scale=picked_s[:],
                 start=True,
                 stop=True,
             )
-        quantise(1, 0, HALF)
+        h_b.append(keep.tile([P, QUARTER * PACK], BF16, name="h_b3", tag="h_b3", align_bytes=64))
+        weave_on_vector(T - QUARTER, QUARTER)
+        quantise(2)
+        quantise(3)
 
         e_sb = keep.tile([P, 2, HALF], F32, name="e_sb", tag="e_sb", align_bytes=64)
 
         def scatter(n):
             d = keep.tile([P, J], F32, name="d%d" % n, tag="d%d" % min(n, 1), align_bytes=64)
-            nc.scalar.activation(d[:], p_first[:] if n == 0 else p_rest[:, n - 1, :], RELU, scale=4.0)
+            nc.scalar.activation(d[:], p[n], RELU, scale=4.0)
             nc.vector.tensor_copy(out=dp[n][:].indirect(offsets[:]), in_=d[:])
 
         def store(queue, n, h):
             queue.dma_start(out=out[P * n : P * (n + 1), h * HALF : (h + 1) * HALF], in_=y[n][h][:])
 
-        def finish_on_gpsimd(n):
+        def finish_on_gpsimd(n, queue):
             nc.scalar.activation(e_sb[:, n // 2, :], e[n, 0][:], COPY)
             nc.gpsimd.tensor_tensor(y[n][0][:], e_sb[:, n // 2, :], dp[n][:, 0:HALF], ADD)
-            store(nc.sync if n == 0 else nc.scalar, n, 0)
+            store(queue, n, 0)
 
         def finish_on_vector(n, h):
             nc.vector.tensor_tensor(y[n][h][:], e[n, h][:], dp[n][:, h * HALF : (h + 1) * HALF], ADD)
@@ -212,14 +232,14 @@ def tile_list_stay_or_leave_kernel(tc, xq_words, xq_scales, w1_words, w1_scales,
         scatter(0)
         e[1, 0] = exit_product(1, 0, 0)
         for n in range(N_TILES):
-            e[n, 1] = exit_product(n, 1, 4 + n)
+            e[n, 1] = exit_product(n, 1, HALF // CHUNK + n)
         scatter(1)
-        finish_on_gpsimd(0)
+        finish_on_gpsimd(0, nc.sync)
         e[2, 0] = exit_product(2, 0, 2)
         finish_on_vector(1, 0)
         finish_on_vector(0, 1)
         scatter(2)
-        finish_on_gpsimd(2)
+        finish_on_gpsimd(2, nc.scalar)
         finish_on_vector(1, 1)
         finish_on_vector(2, 1)
         scatter(3)

from contextlib import ExitStack

import concourse.mybir as mybir

K, T, J, R, N = 512, 1024, 128, 512, 512
FLOPS = 2 * K * R * T + 2 * R * N * T + 2 * R * N * J

F32 = mybir.dt.float32
BF16 = mybir.dt.bfloat16
I32 = mybir.dt.int32
U32 = mybir.dt.uint32
U16 = mybir.dt.uint16
U8 = mybir.dt.uint8
FP8X4 = mybir.dt.float8_e4m3fn_x4
FP4X4 = mybir.dt.float4_e2m1fn_x4
RELU = mybir.ActivationFunctionType.Relu
COPY = mybir.ActivationFunctionType.Copy
ADD = mybir.AluOpType.add

P = 128
PACK = 4
QUADRANT = 32
CHUNK = 128
QUARTER = 256
LINE = 4
HALF = 512
N_TILES = N // P


def load_scale_rows(queue, scale_tile, scales):
    for q in range(P // QUADRANT):
        queue.dma_start(
            out=scale_tile[QUADRANT * q : QUADRANT * q + 4, :].bitcast(I32),
            in_=scales[0, 4 * q : 4 * q + 4, :].bitcast(I32),
        )


def load_scale_quadrant(queue, scale_tile, scales, q):
    rows = scales[0, 4 * q : 4 * q + 4, :].bitcast(I32)
    queue.dma_start(
        out=scale_tile[QUADRANT * q : QUADRANT * (q + 1), :].bitcast(I32),
        in_=rows.partition_broadcast(QUADRANT // 4),
    )


def tile_list_stay_or_leave_kernel(
    tc, xq_words, xq_scales, w1_words, w1_scales, wx_words, wx_scales, wb_words, wb_scales, offs, out
):
    nc = tc.nc
    with ExitStack() as ctx:
        keep = ctx.enter_context(tc.tile_pool(name="keep", bufs=1))
        psum = ctx.enter_context(tc.psum_pool(name="psum", bufs=1))

        offsets = keep.tile([P, J // 16], U16, name="offsets")
        w1_stage = keep.tile([P, 3 * R], U8, name="w1_stage", tag="dp3", align_bytes=64)
        w1_raw_c = w1_stage[:, 0 : 2 * R]
        w1_raw_s = w1_stage[:, 2 * R : 3 * R]
        w1_c = keep.tile([P, 2 * R], U8, name="w1_c", align_bytes=64)
        w1_s = keep.tile([P, R], U8, name="w1_s", align_bytes=64)
        x_c = [keep.tile([P, HALF], U32, name="x_c%d" % h, align_bytes=64) for h in range(2)]
        x_s = keep.tile([P, T], U8, name="x_s", align_bytes=64)
        wx_c = keep.tile([P, N], U32, name="wx_c", align_bytes=64)
        wx_s = keep.tile([P, N], U8, name="wx_s", align_bytes=64)
        wb_c = keep.tile([P, 2 * N], U8, name="wb_c", align_bytes=64)
        wb_s = keep.tile([P, N], U8, name="wb_s", align_bytes=64)
        hid = keep.tile([P, PACK, T], F32, name="hid", align_bytes=64)
        h_b = [keep.tile([P, QUARTER * PACK], BF16, name="h_b%d" % u, align_bytes=64) for u in range(3)]
        h_c = [keep.tile([P, HALF], U32, name="h_c%d" % h, align_bytes=64) for h in range(2)]
        h_s = [keep.tile([P, HALF], U8, name="h_s%d" % h, align_bytes=64) for h in range(2)]
        picked_b = keep.tile([P, J, PACK], BF16, name="picked_b", tag="h_b3", align_bytes=64)
        picked_c = keep.tile([P, J], U32, name="picked_c", tag="e_sb", align_bytes=64)
        picked_s = keep.tile([P, J], U8, name="picked_s", align_bytes=64)
        y = [
            [keep.tile([P, HALF], F32, name="y%d_%d" % (n, h), align_bytes=64) for h in range(2)]
            for n in range(N_TILES)
        ]

        x_bytes = xq_words[0].rearrange("p c r -> p (c r)")
        load_scale_quadrant(nc.sync, w1_raw_s, w1_scales, 0)
        load_scale_quadrant(nc.scalar, x_s, xq_scales, 0)
        load_scale_quadrant(nc.sync, w1_raw_s, w1_scales, 1)
        nc.scalar.dma_start(out=w1_raw_c.bitcast(I32), in_=w1_words[0].bitcast(I32))
        load_scale_quadrant(nc.sync, w1_raw_s, w1_scales, 2)
        load_scale_quadrant(nc.scalar, x_s, xq_scales, 1)
        load_scale_quadrant(nc.sync, w1_raw_s, w1_scales, 3)
        nc.scalar.dma_start(out=x_c[0][:].bitcast(I32), in_=x_bytes[:, 0 : PACK * HALF].bitcast(I32))
        load_scale_quadrant(nc.sync, x_s, xq_scales, 2)
        load_scale_quadrant(nc.sync, x_s, xq_scales, 3)
        nc.gpsimd.memset(wx_s[:].bitcast(I32), 0)
        nc.gpsimd.memset(wb_s[:].bitcast(I32), 0)
        nc.sync.dma_start(out=x_c[1][:].bitcast(I32), in_=x_bytes[:, PACK * HALF : PACK * T].bitcast(I32))
        nc.sync.dma_start(offsets[:], offs)
        nc.sync.dma_start(out=wx_c[:].bitcast(I32), in_=wx_words[0].rearrange("p c r -> p (c r)").bitcast(I32))
        load_scale_rows(nc.sync, wx_s, wx_scales)
        nc.sync.dma_start(out=wb_c[:].bitcast(I32), in_=wb_words[0].bitcast(I32))
        load_scale_rows(nc.sync, wb_s, wb_scales)

        dp = []

        def clear_page(engine, n):
            page = keep.tile([P, T], F32, name="dp%d" % n, tag="dp%d" % n, align_bytes=64)
            engine.memset(page[:].bitcast(I32), 0)
            dp.append(page)

        clear_page(nc.vector, 0)
        clear_page(nc.vector, 1)
        clear_page(nc.gpsimd, 2)

        nc.vector.tensor_copy(
            out=w1_s[:].rearrange("p (j m) -> p j m", j=PACK),
            in_=w1_raw_s.rearrange("p (m j) -> p j m", j=PACK),
        )
        nc.vector.tensor_copy(
            out=w1_c[:].bitcast(U16).rearrange("p (j m) -> p j m", j=PACK),
            in_=w1_raw_c.bitcast(U16).rearrange("p (m j) -> p j m", j=PACK),
        )
        clear_page(nc.vector, 3)

        def bank(b, shape, name):
            return psum.tile(shape, F32, name=name, tag="bank%d" % b)

        def first_product(dst, j, h, start, width):
            nc.tensor.matmul_mx(
                out=dst,
                lhsT=w1_c[:, 2 * P * j : 2 * P * (j + 1)].bitcast(FP4X4),
                lhsT_scale=w1_s[:, P * j : P * (j + 1)],
                rhs=x_c[h][:, start : start + width].bitcast(FP8X4),
                rhs_scale=x_s[:, h * HALF + start : h * HALF + start + width],
                start=True,
                stop=True,
            )

        def woven(first, width):
            u, start = divmod(first, QUARTER)
            return (
                h_b[u][:, PACK * start : PACK * (start + width)].rearrange("p (g i j) -> p g j i", i=LINE, j=PACK),
                hid[:, :, first : first + width].rearrange("p j (g i) -> p g j i", i=LINE),
            )

        def weave_on_vector(first, width):
            dst, src = woven(first, width)
            nc.vector.tensor_copy(out=dst, in_=src)

        def weave_on_scalar(first, width):
            dst, src = woven(first, width)
            nc.scalar.activation(dst, src, COPY)

        def quantise(u):
            h, start = divmod(u * QUARTER, HALF)
            nc.vector.quantize_mx(
                out=h_c[h][:, start : start + QUARTER].bitcast(FP8X4),
                scales=h_s[h][:, start : start + QUARTER],
                in_=h_b[u][:],
            )

        for c in range(HALF // CHUNK):
            acc = bank(c, [P, PACK, CHUNK], "a%d" % c)
            for j in range(PACK):
                first_product(acc[:, j, :], j, 0, c * CHUNK, CHUNK)
            nc.scalar.activation(hid[:, :, c * CHUNK : (c + 1) * CHUNK], acc[:], RELU)
            weave_on_vector(c * CHUNK, CHUNK)
            if c == 2:
                quantise(0)

        for j in range(PACK):
            acc = bank(HALF // CHUNK + j, [P, HALF], "a%d" % (HALF // CHUNK + j))
            first_product(acc[:], j, 1, 0, HALF)
            if j == 0:
                nc.vector.tensor_scalar_max(hid[:, j, HALF:T], acc[:], 0.0)
            else:
                nc.scalar.activation(hid[:, j, HALF:T], acc[:], RELU)
            nc.vector.tensor_copy(out=picked_b[:, :, j], in_=hid[:, j, :].indirect(offsets[:]))
            if j == 0:
                quantise(1)

        def exit_product(n, h, b):
            acc = bank(b, [P, HALF], "e%d_%d" % (n, h))
            nc.tensor.matmul_mx(
                out=acc[:],
                lhsT=wx_c[:, P * n : P * (n + 1)].bitcast(FP8X4),
                lhsT_scale=wx_s[:, P * n : P * (n + 1)],
                rhs=h_c[h][:].bitcast(FP8X4),
                rhs_scale=h_s[h][:],
                start=True,
                stop=True,
            )
            return acc

        e = {(0, 0): exit_product(0, 0, 2)}
        weave_on_scalar(HALF, CHUNK)
        weave_on_scalar(HALF + CHUNK, CHUNK)
        nc.vector.quantize_mx(
            out=picked_c[:].bitcast(FP8X4), scales=picked_s[:], in_=picked_b[:].rearrange("p t j -> p (t j)")
        )
        p_first = bank(0, [P, J], "p_first")
        p_rest = bank(1, [P, N_TILES - 1, J], "p_rest")
        p = [p_first[:]] + [p_rest[:, n, :] for n in range(N_TILES - 1)]
        for n in range(N_TILES):
            nc.tensor.matmul_mx(
                out=p[n],
                lhsT=wb_c[:, 2 * P * n : 2 * P * (n + 1)].bitcast(FP4X4),
                lhsT_scale=wb_s[:, P * n : P * (n + 1)],
                rhs=picked_c[:].bitcast(FP8X4),
                rhs_scale=picked_s[:],
                start=True,
                stop=True,
            )
        h_b.append(keep.tile([P, QUARTER * PACK], BF16, name="h_b3", tag="h_b3", align_bytes=64))
        weave_on_vector(T - QUARTER, QUARTER)
        quantise(2)
        quantise(3)

        e_sb = keep.tile([P, 2, HALF], F32, name="e_sb", tag="e_sb", align_bytes=64)

        def scatter(n):
            d = keep.tile([P, J], F32, name="d%d" % n, tag="d%d" % min(n, 1), align_bytes=64)
            nc.scalar.activation(d[:], p[n], RELU, scale=4.0)
            nc.vector.tensor_copy(out=dp[n][:].indirect(offsets[:]), in_=d[:])

        def store(queue, n, h):
            queue.dma_start(out=out[P * n : P * (n + 1), h * HALF : (h + 1) * HALF], in_=y[n][h][:])

        def finish_on_gpsimd(n, queue):
            nc.scalar.activation(e_sb[:, n // 2, :], e[n, 0][:], COPY)
            nc.gpsimd.tensor_tensor(y[n][0][:], e_sb[:, n // 2, :], dp[n][:, 0:HALF], ADD)
            store(queue, n, 0)

        def finish_on_vector(n, h):
            nc.vector.tensor_tensor(y[n][h][:], e[n, h][:], dp[n][:, h * HALF : (h + 1) * HALF], ADD)
            store(nc.sync, n, h)

        scatter(0)
        e[1, 0] = exit_product(1, 0, 0)
        for n in range(N_TILES):
            e[n, 1] = exit_product(n, 1, HALF // CHUNK + n)
        scatter(1)
        finish_on_gpsimd(0, nc.sync)
        e[2, 0] = exit_product(2, 0, 2)
        finish_on_vector(1, 0)
        finish_on_vector(0, 1)
        scatter(2)
        finish_on_gpsimd(2, nc.scalar)
        finish_on_vector(1, 1)
        finish_on_vector(2, 1)
        scatter(3)
        e[3, 0] = exit_product(3, 0, 1)
        finish_on_vector(3, 1)
        finish_on_vector(3, 0)
